import numpy as np
import ml_dtypes


def mxq(x, axis, fmt="e4m3"):
    dtype, down = {"e4m3": (ml_dtypes.float8_e4m3fn, 7), "e5m2": (ml_dtypes.float8_e5m2, 14)}[fmt]
    v = np.moveaxis(np.asarray(x, np.float32).astype(ml_dtypes.bfloat16).astype(np.float64), axis, -1)
    blocks = v.reshape(v.shape[:-1] + (-1, 32))
    amax = np.abs(blocks).max(-1, keepdims=True)
    byte = np.maximum(np.where(amax > 0, np.frexp(amax)[1] - 1 + 127, 0) - down, 1)
    scale = np.exp2(byte - 127.0)
    codes = (blocks / scale).astype(np.float32).astype(dtype).astype(np.float64)
    return np.moveaxis((codes * scale).reshape(v.shape), -1, axis)


WIDE = False


def mx_kscale(k):
    if not WIDE:
        return np.ones(k)
    levels = np.array([10, -10, 5, -5, 0])
    if k % 512:
        return np.exp2(np.random.permutation(np.resize(levels, k // 32))).repeat(32)
    a = np.empty((k // 512, 16))
    for p in range(k // 512):
        a[p, :8] = np.random.permutation(np.resize(levels, 8))
        for g in range(8):
            far = levels[np.abs(levels - a[p, g]) >= 10]
            a[p, g + 8] = far[np.random.randint(len(far))]
    return np.exp2(a.ravel()).repeat(32)


def f64(x):
    return np.asarray(x).astype(np.float64)


def striped(idx):
    return np.tile(idx.reshape(-1, 16).T, (8, 1)).astype(np.uint16)


def unstriped(offs):
    return offs[:16].T.reshape(-1).astype(np.int64)


def striped8(idx):
    return np.concatenate([x.reshape(-1, 16).T for x in idx]).astype(np.uint16)


def runs(offs, k):
    lists = np.stack([offs[16 * r : 16 * r + 16].T.reshape(-1) for r in range(8)]).astype(np.int64)
    return lists[np.arange(k) % 512 // 64]


def pack_weight(w):
    k, n = w.shape
    w = f64(np.asarray(w, np.float32).astype(ml_dtypes.bfloat16)).reshape(k // 32, 32, n)
    amax = np.abs(w).max(1)
    byte = np.clip(np.where(amax > 0, np.frexp(amax)[1] - 1 + 127 - 7, 1), 1, 254)
    scaled = (w * np.exp2(127.0 - byte)[:, None, :]).reshape(k, n).astype(np.float32)
    words = np.ascontiguousarray(scaled.reshape(k // 512, 128, 4, n).transpose(0, 1, 3, 2)).astype(ml_dtypes.float8_e4m3fn).view(np.uint8)
    return words, np.ascontiguousarray(byte.astype(np.uint8).reshape(k // 512, 16, n))


def unpack_weight(words, scales):
    g, p, n, _ = words.shape
    vals = np.ascontiguousarray(words).view(ml_dtypes.float8_e4m3fn).astype(np.float64) * np.repeat(np.exp2(scales.astype(np.float64) - 127.0), 8, axis=1)[..., None]
    return vals.transpose(0, 1, 3, 2).reshape(g * 512, n)


def sigmoid(v):
    return 1.0 / (1.0 + np.exp(-np.maximum(v, -700.0)))


K, T, S, N, H = 512, 2048, 512, 512, 512


def setup_inputs():
    n = np.random.standard_normal
    s = mx_kscale(K)[:, None]
    u = mx_kscale(H)
    packed_xT = pack_weight(n((K, T)) * s)
    return {
        "x_words": packed_xT[0],
        "x_scales": packed_xT[1],
        "w1": (n((K, H)) / np.sqrt(K) / s).astype(np.float32),
        "gn": (np.random.uniform(0.5, 1.5, (H, 1)) * u[:, None]).astype(np.float32),
        "w2": (n((H, N)) / np.sqrt(H) / u[:, None]).astype(np.float32),
        "w3": (n((K, N)) / np.sqrt(K) / s).astype(np.float32),
        "offs": striped(np.random.permutation(T)[:S]),
        "n1": striped8(np.stack([np.random.permutation(S) for _ in range(8)])),
        "n2": striped8(np.stack([np.random.permutation(S) for _ in range(8)])),
        "two": striped(np.random.permutation(T)[:S]),
        "n3": striped8(np.stack([np.random.permutation(S) for _ in range(8)])),
        "n4": striped8(np.stack([np.random.permutation(S) for _ in range(8)])),
        "n5": striped8(np.stack([np.random.permutation(S) for _ in range(8)])),
    }


def reference(x_words, x_scales, w1, gn, w2, w3, offs, n1, n2, two, n3, n4, n5):
    xq = unpack_weight(x_words, x_scales)[:, unstriped(offs)]
    y = mxq(f64(w1), 0, "e4m3").T @ xq
    st = y[np.arange(H)[:, None], runs(n1, H)] - y
    z = f64(gn) * (y * (sigmoid(st[np.arange(H)[:, None], runs(n2, H)])))
    h = mxq(f64(w2), 0, "e4m3").T @ mxq(z, 0, "e4m3")
    x_two = unpack_weight(x_words, x_scales)[:, unstriped(two)]
    d = mxq(f64(w3), 0, "e4m3").T @ x_two
    return np.maximum(np.minimum(h - (0.5 * (h[np.arange(N)[:, None], runs(n3, N)])), d[np.arange(N)[:, None], runs(n4, N)]), d[np.arange(N)[:, None], runs(n5, N)])

@@ -1,0 +1,158 @@
+from contextlib import ExitStack
+
+import concourse.mybir as mybir
+
+K, T, S, N, H = 512, 2048, 512, 512, 512
+FLOPS = 3 * 2 * 512 * 512 * 512
+
+F32 = mybir.dt.float32
+BF16 = mybir.dt.bfloat16
+I32 = mybir.dt.int32
+U32 = mybir.dt.uint32
+U16 = mybir.dt.uint16
+U8 = mybir.dt.uint8
+FP8X4 = mybir.dt.float8_e4m3fn_x4
+ALU = mybir.AluOpType
+ACT = mybir.ActivationFunctionType
+
+P = 128
+PACK = 4
+WIN = 2 * S
+
+
+def tile_picked_lateclampbhopd_none_p_kernel(tc, x_words, x_scales, w1, gn, w2, w3, offs, n1, n2, two, n3, n4, n5, out):
+    nc = tc.nc
+    with ExitStack() as ctx:
+        keep = ctx.enter_context(tc.tile_pool(name="keep", bufs=1))
+        psum = ctx.enter_context(tc.psum_pool(name="psum", bufs=1))
+
+        def load_list(name, src):
+            tile = keep.tile([P, S // 16], U16, name=name)
+            nc.sync.dma_start(tile[:], src)
+            return tile
+
+        def load_weight(name, src):
+            tile = keep.tile([P, PACK, src.shape[1]], F32, name=name, align_bytes=64)
+            nc.sync.dma_start(tile[:], src.rearrange("(p j) c -> p j c", j=PACK))
+            return tile
+
+        scale_table = keep.tile([P, T], U8, name="scale_table", align_bytes=64)
+        nc.vector.memset(scale_table[:].bitcast(I32), 0)
+        offs_t = load_list("offs_t", offs)
+        w1_left = load_weight("w1_left", w1[:, :256])
+        for q in range(4):
+            nc.sync.dma_start(scale_table[32 * q : 32 * q + 4, :].bitcast(I32), x_scales[0, 4 * q : 4 * q + 4, :].bitcast(I32))
+        two_t = load_list("two_t", two)
+        warm = keep.tile([P, 2], F32, name="warm")
+        nc.vector.memset(warm[:, 0:1], 0.0)
+        nc.scalar.activation(warm[:, 1:2], warm[:, 0:1], ACT.Sigmoid)
+        w1_right = load_weight("w1_right", w1[:, 256:])
+        word_table = keep.tile([P, T], U32, name="word_table", align_bytes=64)
+        nc.sync.dma_start(word_table[:].bitcast(I32), x_words[0].rearrange("p n t -> p (n t)").bitcast(I32))
+        w3_raw = load_weight("w3_raw", w3)
+        n1_t = load_list("n1_t", n1)
+        n2_t = load_list("n2_t", n2)
+        gain = keep.tile([P, PACK], F32, name="gain")
+        nc.sync.dma_start(gain[:], gn.rearrange("(p t) o -> p (t o)", t=PACK))
+        n4_t = load_list("n4_t", n4)
+        n5_t = load_list("n5_t", n5)
+        w2_raw = load_weight("w2_raw", w2)
+        n3_t = load_list("n3_t", n3)
+
+        def pick(name, table, dtype, index):
+            tile = keep.tile([P, S], dtype, name=name, align_bytes=64)
+            nc.vector.tensor_copy(tile[:], table[:].indirect(index[:]))
+            return tile
+
+        def deal(name, parts, copy):
+            dealt = keep.tile([P, PACK * 512], BF16, name=name, align_bytes=64)
+            view = dealt[:].rearrange("p (t m j) -> p m j t", t=PACK, j=PACK)
+            width = P // len(parts)
+            for i, raw in enumerate(parts):
+                copy(view[:, i * width : (i + 1) * width], raw[:].rearrange("p j (m t) -> p m j t", t=PACK))
+            return dealt
+
+        def quantize(name, values):
+            codes = keep.tile([P, 512], U32, name=name + "_codes", align_bytes=64)
+            scales = keep.tile([P, 512], U8, name=name + "_scales", align_bytes=64)
+            nc.vector.quantize_mx(out=codes[:].bitcast(FP8X4), scales=scales[:], in_=values[:])
+            return codes, scales
+
+        def product(tag, weights, moving):
+            banks = []
+            for t in range(PACK):
+                bank = psum.tile([P, S], F32, name=f"{tag}{t}", tag=f"{tag}{t}")
+                cols = slice(P * t, P * (t + 1))
+                nc.tensor.matmul_mx(out=bank[:], lhsT=weights[0][:, cols].bitcast(FP8X4), lhsT_scale=weights[1][:, cols],
+                                    rhs=moving[0][:].bitcast(FP8X4), rhs_scale=moving[1][:], start=True, stop=True)
+                banks.append(bank)
+            return banks
+
+        def windows(name):
+            return [keep.tile([P, WIN], F32, name=f"{name}{t}", align_bytes=64) for t in range(PACK)]
+
+        x1_scales = pick("x1_scales", scale_table, U8, offs_t)
+        x2_scales = pick("x2_scales", scale_table, U8, two_t)
+        w1_q = quantize("w1", deal("w1_dealt", [w1_left, w1_right], nc.scalar.copy))
+        x1_words = pick("x1_words", word_table, U32, offs_t)
+        y_banks = product("a", w1_q, (x1_words, x1_scales))
+        x2_words = pick("x2_words", word_table, U32, two_t)
+        w3_q = quantize("w3", deal("w3_dealt", [w3_raw], nc.vector.tensor_copy))
+        d_banks = product("b", w3_q, (x2_words, x2_scales))
+
+        y_win, st_win, d_win, h_win = windows("y_win"), windows("st_win"), windows("d_win"), windows("h_win")
+        y_plain = keep.tile([P, PACK, S], F32, name="y_plain", align_bytes=64)
+        for t in range(PACK):
+            nc.scalar.copy(y_win[t][:, :S], y_banks[t][:])
+            nc.scalar.copy(y_plain[:, t, :], y_banks[t][:])
+            nc.vector.tensor_tensor(st_win[t][:, :S], y_win[t][:].indirect(n1_t[:]), y_plain[:, t, :], ALU.subtract)
+        for t in range(PACK):
+            nc.scalar.copy(d_win[t][:, :S], d_banks[t][:])
+        gate = keep.tile([P, PACK, S], F32, name="gate", align_bytes=64)
+        y_gained = keep.tile([P, PACK, S], F32, name="y_gained", align_bytes=64)
+        for t in range(PACK):
+            nc.scalar.activation(gate[:, t, :], st_win[t][:].indirect(n2_t[:]), ACT.Sigmoid)
+        for t in range(PACK):
+            nc.scalar.activation(y_gained[:, t, :], y_banks[t][:], ACT.Copy, scale=gain[:, t : t + 1])
+        w2_dealt = deal("w2_dealt", [w2_raw], nc.scalar.copy)
+
+        d4 = keep.tile([P, PACK, S], F32, name="d4", align_bytes=64)
+        d5 = keep.tile([P, PACK, S], F32, name="d5", align_bytes=64)
+        for t in range(PACK - 1):
+            nc.vector.tensor_copy(d4[:, t, :], d_win[t][:].indirect(n4_t[:]))
+            nc.vector.tensor_copy(d5[:, t, :], d_win[t][:].indirect(n5_t[:]))
+
+        z = keep.tile([P, PACK * S], BF16, name="z", tag="z", align_bytes=64)
+        nc.vector.tensor_tensor(
+            z[:].rearrange("p (c i t) -> p c t i", i=4, t=PACK),
+            y_gained[:].rearrange("p t (c i) -> p c t i", i=4),
+            gate[:].rearrange("p t (c i) -> p c t i", i=4),
+            ALU.mult,
+        )
+        w2_q = quantize("w2", w2_dealt)
+        z_q = quantize("z", z)
+        h_banks = product("a", w2_q, z_q)
+        t = PACK - 1
+        late = keep.tile([P, 2, S], F32, name="late", tag="z", align_bytes=64)
+        nc.vector.tensor_copy(late[:, 0, :], d_win[t][:].indirect(n4_t[:]))
+        nc.vector.tensor_copy(late[:, 1, :], d_win[t][:].indirect(n5_t[:]))
+        cap = [d4[:, t, :] for t in range(PACK - 1)] + [late[:, 0, :]]
+        floor = [d5[:, t, :] for t in range(PACK - 1)] + [late[:, 1, :]]
+
+        h_plain = keep.tile([P, PACK, S], F32, name="h_plain", align_bytes=64)
+        pulled = keep.tile([P, PACK, S], F32, name="pulled", align_bytes=64)
+        capped = keep.tile([P, PACK, S], F32, name="capped", align_bytes=64)
+        result = keep.tile([P, PACK, S], F32, name="result", align_bytes=64)
+        out_rows = out.rearrange("(p t) j -> p t j", t=PACK)
+        for t in range(PACK):
+            nc.scalar.activation(h_win[t][:, :S], h_banks[t][:], ACT.Copy, scale=-0.5)
+            nc.scalar.copy(h_plain[:, t, :], h_banks[t][:])
+        for step in range(PACK + 1):
+            if step < PACK:
+                nc.vector.tensor_tensor(pulled[:, step, :], h_win[step][:].indirect(n3_t[:]), h_plain[:, step, :], ALU.add)
+            if step >= 1:
+                t = step - 1
+                nc.vector.tensor_tensor(result[:, t, :], capped[:, t, :], floor[t], ALU.max)
+                nc.sync.dma_start(out_rows[:, t, :], result[:, t, :])
+            if step < PACK:
+                nc.vector.tensor_tensor(capped[:, step, :], pulled[:, step, :], cap[step], ALU.min)

@@ -64,11 +64,11 @@ def tile_picked_lateclampbhopd_none_p_kernel(tc, x_words, x_scales, w1, gn, w2, 
             nc.vector.tensor_copy(tile[:], table[:].indirect(index[:]))
             return tile
 
-        def deal(name, parts, copy):
-            dealt = keep.tile([P, PACK * 512], BF16, name=name, align_bytes=64)
+        def deal(name, parts):
+            dealt = keep.tile([P, PACK * 512], BF16, name=name, tag=name, align_bytes=64)
             view = dealt[:].rearrange("p (t m j) -> p m j t", t=PACK, j=PACK)
             width = P // len(parts)
-            for i, raw in enumerate(parts):
+            for i, (raw, copy) in enumerate(parts):
                 copy(view[:, i * width : (i + 1) * width], raw[:].rearrange("p j (m t) -> p m j t", t=PACK))
             return dealt
 
@@ -93,12 +93,11 @@ def tile_picked_lateclampbhopd_none_p_kernel(tc, x_words, x_scales, w1, gn, w2, 
 
         x1_scales = pick("x1_scales", scale_table, U8, offs_t)
         x2_scales = pick("x2_scales", scale_table, U8, two_t)
-        w1_q = quantize("w1", deal("w1_dealt", [w1_left, w1_right], nc.scalar.copy))
+        w1_q = quantize("w1", deal("w1_dealt", [(w1_left, nc.scalar.copy), (w1_right, nc.scalar.copy)]))
         x1_words = pick("x1_words", word_table, U32, offs_t)
         y_banks = product("a", w1_q, (x1_words, x1_scales))
         x2_words = pick("x2_words", word_table, U32, two_t)
-        w3_q = quantize("w3", deal("w3_dealt", [w3_raw], nc.vector.tensor_copy))
-        d_banks = product("b", w3_q, (x2_words, x2_scales))
+        w3_dealt = deal("w3_dealt", [(w3_raw, nc.vector.tensor_copy)])
 
         y_win, st_win, d_win, h_win = windows("y_win"), windows("st_win"), windows("d_win"), windows("h_win")
         y_plain = keep.tile([P, PACK, S], F32, name="y_plain", align_bytes=64)
@@ -106,7 +105,9 @@ def tile_picked_lateclampbhopd_none_p_kernel(tc, x_words, x_scales, w1, gn, w2, 
             nc.scalar.copy(y_win[t][:, :S], y_banks[t][:])
             nc.scalar.copy(y_plain[:, t, :], y_banks[t][:])
             nc.vector.tensor_tensor(st_win[t][:, :S], y_win[t][:].indirect(n1_t[:]), y_plain[:, t, :], ALU.subtract)
-        for t in range(PACK):
+            if t == 0:
+                d_banks = product("b", quantize("w3", w3_dealt), (x2_words, x2_scales))
+        for t in range(PACK - 1):
             nc.scalar.copy(d_win[t][:, :S], d_banks[t][:])
         gate = keep.tile([P, PACK, S], F32, name="gate", align_bytes=64)
         y_gained = keep.tile([P, PACK, S], F32, name="y_gained", align_bytes=64)
@@ -114,7 +115,8 @@ def tile_picked_lateclampbhopd_none_p_kernel(tc, x_words, x_scales, w1, gn, w2, 
             nc.scalar.activation(gate[:, t, :], st_win[t][:].indirect(n2_t[:]), ACT.Sigmoid)
         for t in range(PACK):
             nc.scalar.activation(y_gained[:, t, :], y_banks[t][:], ACT.Copy, scale=gain[:, t : t + 1])
-        w2_dealt = deal("w2_dealt", [w2_raw], nc.scalar.copy)
+        w2_dealt = deal("w2_dealt", [(w2_raw, nc.scalar.copy)])
+        nc.scalar.copy(d_win[PACK - 1][:, :S], d_banks[PACK - 1][:])
 
         d4 = keep.tile([P, PACK, S], F32, name="d4", align_bytes=64)
         d5 = keep.tile([P, PACK, S], F32, name="d5", align_bytes=64)
@@ -123,21 +125,23 @@ def tile_picked_lateclampbhopd_none_p_kernel(tc, x_words, x_scales, w1, gn, w2, 
             nc.vector.tensor_copy(d5[:, t, :], d_win[t][:].indirect(n5_t[:]))
 
         z = keep.tile([P, PACK * S], BF16, name="z", tag="z", align_bytes=64)
-        nc.vector.tensor_tensor(
-            z[:].rearrange("p (c i t) -> p c t i", i=4, t=PACK),
-            y_gained[:].rearrange("p t (c i) -> p c t i", i=4),
-            gate[:].rearrange("p t (c i) -> p c t i", i=4),
-            ALU.mult,
-        )
-        w2_q = quantize("w2", w2_dealt)
-        z_q = quantize("z", z)
-        h_banks = product("a", w2_q, z_q)
-        t = PACK - 1
+        z_codes = keep.tile([P, S], U32, name="z_codes", align_bytes=64)
+        z_scales = keep.tile([P, S], U8, name="z_scales", align_bytes=64)
+        halves = [slice(0, S // 2), slice(S // 2, S)]
+        for cols in halves:
+            nc.vector.tensor_tensor(
+                z[:, PACK * cols.start : PACK * cols.stop].rearrange("p (c i t) -> p c t i", i=4, t=PACK),
+                y_gained[:, :, cols].rearrange("p t (c i) -> p c t i", i=4),
+                gate[:, :, cols].rearrange("p t (c i) -> p c t i", i=4),
+                ALU.mult,
+            )
+        for cols in halves:
+            nc.vector.quantize_mx(out=z_codes[:, cols].bitcast(FP8X4), scales=z_scales[:, cols], in_=z[:, PACK * cols.start : PACK * cols.stop])
+        h_banks = product("a", quantize("w2", w2_dealt), (z_codes, z_scales))
+
         late = keep.tile([P, 2, S], F32, name="late", tag="z", align_bytes=64)
-        nc.vector.tensor_copy(late[:, 0, :], d_win[t][:].indirect(n4_t[:]))
-        nc.vector.tensor_copy(late[:, 1, :], d_win[t][:].indirect(n5_t[:]))
-        cap = [d4[:, t, :] for t in range(PACK - 1)] + [late[:, 0, :]]
-        floor = [d5[:, t, :] for t in range(PACK - 1)] + [late[:, 1, :]]
+        nc.vector.tensor_copy(late[:, 0, :], d_win[PACK - 1][:].indirect(n4_t[:]))
+        nc.vector.tensor_copy(late[:, 1, :], d_win[PACK - 1][:].indirect(n5_t[:]))
 
         h_plain = keep.tile([P, PACK, S], F32, name="h_plain", align_bytes=64)
         pulled = keep.tile([P, PACK, S], F32, name="pulled", align_bytes=64)
@@ -147,12 +151,21 @@ def tile_picked_lateclampbhopd_none_p_kernel(tc, x_words, x_scales, w1, gn, w2, 
         for t in range(PACK):
             nc.scalar.activation(h_win[t][:, :S], h_banks[t][:], ACT.Copy, scale=-0.5)
             nc.scalar.copy(h_plain[:, t, :], h_banks[t][:])
-        for step in range(PACK + 1):
-            if step < PACK:
-                nc.vector.tensor_tensor(pulled[:, step, :], h_win[step][:].indirect(n3_t[:]), h_plain[:, step, :], ALU.add)
-            if step >= 1:
-                t = step - 1
-                nc.vector.tensor_tensor(result[:, t, :], capped[:, t, :], floor[t], ALU.max)
-                nc.sync.dma_start(out_rows[:, t, :], result[:, t, :])
-            if step < PACK:
-                nc.vector.tensor_tensor(capped[:, step, :], pulled[:, step, :], cap[step], ALU.min)
+
+        def pull(t):
+            nc.vector.tensor_tensor(pulled[:, t, :], h_win[t][:].indirect(n3_t[:]), h_plain[:, t, :], ALU.add)
+
+        pull(0)
+        pull(1)
+        nc.vector.tensor_tensor(capped[:, 0:2, :], pulled[:, 0:2, :], d4[:, 0:2, :], ALU.min)
+        pull(2)
+        nc.vector.tensor_tensor(result[:, 0:2, :], capped[:, 0:2, :], d5[:, 0:2, :], ALU.max)
+        nc.sync.dma_start(out_rows[:, 0:2, :], result[:, 0:2, :])
+        pull(3)
+        nc.vector.tensor_tensor(capped[:, 2, :], pulled[:, 2, :], d4[:, 2, :], ALU.min)
+        nc.vector.tensor_tensor(capped[:, 3, :], pulled[:, 3, :], late[:, 0, :], ALU.min)
+        nc.vector.tensor_tensor(result[:, 2, :], capped[:, 2, :], d5[:, 2, :], ALU.max)
+        nc.sync.dma_start(out_rows[:, 2, :], result[:, 2, :])
+        for cols in halves:
+            nc.vector.tensor_tensor(result[:, 3, cols], capped[:, 3, cols], late[:, 1, cols], ALU.max)
+            nc.sync.dma_start(out_rows[:, 3, cols], result[:, 3, cols])

from contextlib import ExitStack

import concourse.mybir as mybir

K, T, S, N, H = 512, 2048, 512, 512, 512
FLOPS = 3 * 2 * 512 * 512 * 512

F32 = mybir.dt.float32
BF16 = mybir.dt.bfloat16
I32 = mybir.dt.int32
U32 = mybir.dt.uint32
U16 = mybir.dt.uint16
U8 = mybir.dt.uint8
FP8X4 = mybir.dt.float8_e4m3fn_x4
ALU = mybir.AluOpType
ACT = mybir.ActivationFunctionType

P = 128
PACK = 4
WIN = 2 * S


def tile_picked_lateclampbhopd_none_p_kernel(tc, x_words, x_scales, w1, gn, w2, w3, offs, n1, n2, two, n3, n4, n5, out):
    nc = tc.nc
    with ExitStack() as ctx:
        keep = ctx.enter_context(tc.tile_pool(name="keep", bufs=1))
        psum = ctx.enter_context(tc.psum_pool(name="psum", bufs=1))

        def load_list(name, src):
            tile = keep.tile([P, S // 16], U16, name=name)
            nc.sync.dma_start(tile[:], src)
            return tile

        def load_weight(name, src):
            tile = keep.tile([P, PACK, src.shape[1]], F32, name=name, align_bytes=64)
            nc.sync.dma_start(tile[:], src.rearrange("(p j) c -> p j c", j=PACK))
            return tile

        scale_table = keep.tile([P, T], U8, name="scale_table", align_bytes=64)
        nc.vector.memset(scale_table[:].bitcast(I32), 0)
        offs_t = load_list("offs_t", offs)
        w1_left = load_weight("w1_left", w1[:, :256])
        for q in range(4):
            nc.sync.dma_start(scale_table[32 * q : 32 * q + 4, :].bitcast(I32), x_scales[0, 4 * q : 4 * q + 4, :].bitcast(I32))
        two_t = load_list("two_t", two)
        warm = keep.tile([P, 2], F32, name="warm")
        nc.vector.memset(warm[:, 0:1], 0.0)
        nc.scalar.activation(warm[:, 1:2], warm[:, 0:1], ACT.Sigmoid)
        w1_right = load_weight("w1_right", w1[:, 256:])
        word_table = keep.tile([P, T], U32, name="word_table", align_bytes=64)
        nc.sync.dma_start(word_table[:].bitcast(I32), x_words[0].rearrange("p n t -> p (n t)").bitcast(I32))
        w3_raw = load_weight("w3_raw", w3)
        n1_t = load_list("n1_t", n1)
        n2_t = load_list("n2_t", n2)
        gain = keep.tile([P, PACK], F32, name="gain")
        nc.sync.dma_start(gain[:], gn.rearrange("(p t) o -> p (t o)", t=PACK))
        n4_t = load_list("n4_t", n4)
        n5_t = load_list("n5_t", n5)
        w2_raw = load_weight("w2_raw", w2)
        n3_t = load_list("n3_t", n3)

        def pick(name, table, dtype, index):
            tile = keep.tile([P, S], dtype, name=name, align_bytes=64)
            nc.vector.tensor_copy(tile[:], table[:].indirect(index[:]))
            return tile

        def deal(name, parts):
            dealt = keep.tile([P, PACK * 512], BF16, name=name, tag=name, align_bytes=64)
            view = dealt[:].rearrange("p (t m j) -> p m j t", t=PACK, j=PACK)
            width = P // len(parts)
            for i, (raw, copy) in enumerate(parts):
                copy(view[:, i * width : (i + 1) * width], raw[:].rearrange("p j (m t) -> p m j t", t=PACK))
            return dealt

        def quantize(name, values):
            codes = keep.tile([P, 512], U32, name=name + "_codes", align_bytes=64)
            scales = keep.tile([P, 512], U8, name=name + "_scales", align_bytes=64)
            nc.vector.quantize_mx(out=codes[:].bitcast(FP8X4), scales=scales[:], in_=values[:])
            return codes, scales

        def product(tag, weights, moving):
            banks = []
            for t in range(PACK):
                bank = psum.tile([P, S], F32, name=f"{tag}{t}", tag=f"{tag}{t}")
                cols = slice(P * t, P * (t + 1))
                nc.tensor.matmul_mx(out=bank[:], lhsT=weights[0][:, cols].bitcast(FP8X4), lhsT_scale=weights[1][:, cols],
                                    rhs=moving[0][:].bitcast(FP8X4), rhs_scale=moving[1][:], start=True, stop=True)
                banks.append(bank)
            return banks

        def windows(name):
            return [keep.tile([P, WIN], F32, name=f"{name}{t}", align_bytes=64) for t in range(PACK)]

        x1_scales = pick("x1_scales", scale_table, U8, offs_t)
        x2_scales = pick("x2_scales", scale_table, U8, two_t)
        w1_q = quantize("w1", deal("w1_dealt", [(w1_left, nc.scalar.copy), (w1_right, nc.scalar.copy)]))
        x1_words = pick("x1_words", word_table, U32, offs_t)
        y_banks = product("a", w1_q, (x1_words, x1_scales))
        x2_words = pick("x2_words", word_table, U32, two_t)
        w3_dealt = deal("w3_dealt", [(w3_raw, nc.vector.tensor_copy)])

        y_win, st_win, d_win, h_win = windows("y_win"), windows("st_win"), windows("d_win"), windows("h_win")
        y_plain = keep.tile([P, PACK, S], F32, name="y_plain", align_bytes=64)
        for t in range(PACK):
            nc.scalar.copy(y_win[t][:, :S], y_banks[t][:])
            nc.scalar.copy(y_plain[:, t, :], y_banks[t][:])
            nc.vector.tensor_tensor(st_win[t][:, :S], y_win[t][:].indirect(n1_t[:]), y_plain[:, t, :], ALU.subtract)
            if t == 0:
                d_banks = product("b", quantize("w3", w3_dealt), (x2_words, x2_scales))
        for t in range(PACK - 1):
            nc.scalar.copy(d_win[t][:, :S], d_banks[t][:])
        gate = keep.tile([P, PACK, S], F32, name="gate", align_bytes=64)
        y_gained = keep.tile([P, PACK, S], F32, name="y_gained", align_bytes=64)
        for t in range(PACK):
            nc.scalar.activation(gate[:, t, :], st_win[t][:].indirect(n2_t[:]), ACT.Sigmoid)
        for t in range(PACK):
            nc.scalar.activation(y_gained[:, t, :], y_banks[t][:], ACT.Copy, scale=gain[:, t : t + 1])
        w2_dealt = deal("w2_dealt", [(w2_raw, nc.scalar.copy)])
        nc.scalar.copy(d_win[PACK - 1][:, :S], d_banks[PACK - 1][:])

        d4 = keep.tile([P, PACK, S], F32, name="d4", align_bytes=64)
        d5 = keep.tile([P, PACK, S], F32, name="d5", align_bytes=64)
        for t in range(PACK - 1):
            nc.vector.tensor_copy(d4[:, t, :], d_win[t][:].indirect(n4_t[:]))
            nc.vector.tensor_copy(d5[:, t, :], d_win[t][:].indirect(n5_t[:]))

        z = keep.tile([P, PACK * S], BF16, name="z", tag="z", align_bytes=64)
        z_codes = keep.tile([P, S], U32, name="z_codes", align_bytes=64)
        z_scales = keep.tile([P, S], U8, name="z_scales", align_bytes=64)
        halves = [slice(0, S // 2), slice(S // 2, S)]
        for cols in halves:
            nc.vector.tensor_tensor(
                z[:, PACK * cols.start : PACK * cols.stop].rearrange("p (c i t) -> p c t i", i=4, t=PACK),
                y_gained[:, :, cols].rearrange("p t (c i) -> p c t i", i=4),
                gate[:, :, cols].rearrange("p t (c i) -> p c t i", i=4),
                ALU.mult,
            )
        for cols in halves:
            nc.vector.quantize_mx(out=z_codes[:, cols].bitcast(FP8X4), scales=z_scales[:, cols], in_=z[:, PACK * cols.start : PACK * cols.stop])
        h_banks = product("a", quantize("w2", w2_dealt), (z_codes, z_scales))

        late = keep.tile([P, 2, S], F32, name="late", tag="z", align_bytes=64)
        nc.vector.tensor_copy(late[:, 0, :], d_win[PACK - 1][:].indirect(n4_t[:]))
        nc.vector.tensor_copy(late[:, 1, :], d_win[PACK - 1][:].indirect(n5_t[:]))

        h_plain = keep.tile([P, PACK, S], F32, name="h_plain", align_bytes=64)
        pulled = keep.tile([P, PACK, S], F32, name="pulled", align_bytes=64)
        capped = keep.tile([P, PACK, S], F32, name="capped", align_bytes=64)
        result = keep.tile([P, PACK, S], F32, name="result", align_bytes=64)
        out_rows = out.rearrange("(p t) j -> p t j", t=PACK)
        for t in range(PACK):
            nc.scalar.activation(h_win[t][:, :S], h_banks[t][:], ACT.Copy, scale=-0.5)
            nc.scalar.copy(h_plain[:, t, :], h_banks[t][:])

        def pull(t):
            nc.vector.tensor_tensor(pulled[:, t, :], h_win[t][:].indirect(n3_t[:]), h_plain[:, t, :], ALU.add)

        pull(0)
        pull(1)
        nc.vector.tensor_tensor(capped[:, 0:2, :], pulled[:, 0:2, :], d4[:, 0:2, :], ALU.min)
        pull(2)
        nc.vector.tensor_tensor(result[:, 0:2, :], capped[:, 0:2, :], d5[:, 0:2, :], ALU.max)
        nc.sync.dma_start(out_rows[:, 0:2, :], result[:, 0:2, :])
        pull(3)
        nc.vector.tensor_tensor(capped[:, 2, :], pulled[:, 2, :], d4[:, 2, :], ALU.min)
        nc.vector.tensor_tensor(capped[:, 3, :], pulled[:, 3, :], late[:, 0, :], ALU.min)
        nc.vector.tensor_tensor(result[:, 2, :], capped[:, 2, :], d5[:, 2, :], ALU.max)
        nc.sync.dma_start(out_rows[:, 2, :], result[:, 2, :])
        for cols in halves:
            nc.vector.tensor_tensor(result[:, 3, cols], capped[:, 3, cols], late[:, 1, cols], ALU.max)
            nc.sync.dma_start(out_rows[:, 3, cols], result[:, 3, cols])
